import numpy as np
import ml_dtypes


def mxq(x, axis, fmt="e4m3"):
    dtype, down = {"e4m3": (ml_dtypes.float8_e4m3fn, 7), "e5m2": (ml_dtypes.float8_e5m2, 14)}[fmt]
    v = np.moveaxis(np.asarray(x, np.float32).astype(ml_dtypes.bfloat16).astype(np.float64), axis, -1)
    blocks = v.reshape(v.shape[:-1] + (-1, 32))
    amax = np.abs(blocks).max(-1, keepdims=True)
    byte = np.maximum(np.where(amax > 0, np.frexp(amax)[1] - 1 + 127, 0) - down, 1)
    scale = np.exp2(byte - 127.0)
    codes = (blocks / scale).astype(np.float32).astype(dtype).astype(np.float64)
    return np.moveaxis((codes * scale).reshape(v.shape), -1, axis)


WIDE = False


def mx_kscale(k):
    if not WIDE:
        return np.ones(k)
    levels = np.array([10, -10, 5, -5, 0])
    if k % 512:
        return np.exp2(np.random.permutation(np.resize(levels, k // 32))).repeat(32)
    a = np.empty((k // 512, 16))
    for p in range(k // 512):
        a[p, :8] = np.random.permutation(np.resize(levels, 8))
        for g in range(8):
            far = levels[np.abs(levels - a[p, g]) >= 10]
            a[p, g + 8] = far[np.random.randint(len(far))]
    return np.exp2(a.ravel()).repeat(32)


BF16 = ml_dtypes.bfloat16


def bf(x):
    return np.asarray(x, np.float32).astype(BF16)


def f64(x):
    return np.asarray(x).astype(np.float64)


H, N, T, D, R, DV = 2, 512, 1024, 512, 512, 512


def draw0():
    s, t, u = mx_kscale(D), mx_kscale(T), mx_kscale(R)
    return {
        "q": bf(np.random.standard_normal((H, N, D)) * np.random.uniform(0.5, 1.2, (H, N, 1)) * s),
        "k": bf(np.random.standard_normal((H, T, D)) / s),
        "v": bf(np.random.standard_normal((H, T, DV)) / np.sqrt(T) / t[:, None]),
        "g_v": bf(np.random.standard_normal((H, T)) * t),
        "w_phi": bf(np.random.standard_normal((H, D, R)) / np.sqrt(D) / s[:, None]),
        "state": bf(2.0 * np.random.standard_normal((H, R, DV)) / np.sqrt(R) / u[:, None]),
        "g_s": bf(np.random.standard_normal((H, R)) * u),
    }


def core(q, k, v, g_v, w_phi, state, g_s):
    qq = mxq(f64(q), 2, "e4m3")
    a = np.exp((qq @ mxq(f64(k), 2, "e4m3").transpose(0, 2, 1)) / np.sqrt(D))
    phi = np.abs(qq @ mxq(f64(w_phi), 1, "e4m3"))
    ag = a * f64(g_v)[:, None, :]
    pg = phi * f64(g_s)[:, None, :]
    num = (mxq(ag, 2, "e4m3") @ mxq(f64(v), 1, "e4m3")) + (mxq(pg, 2, "e4m3") @ mxq(f64(state), 1, "e4m3"))
    den = np.mean(a, axis=-1) + np.mean(phi, axis=-1)
    return num / den[:, :, None]


def e4m3fn_bytes(y):
    return np.clip(np.asarray(y, np.float64), -448.0, 448.0).astype(np.float32).astype(ml_dtypes.float8_e4m3fn).view(np.uint8)


def e4m3fn_values(b):
    return np.asarray(b, np.uint8).view(ml_dtypes.float8_e4m3fn).astype(np.float64)


def setup_inputs():
    d = draw0()
    x0 = np.asarray(d['v']).astype(np.float64)
    s = (np.max(np.abs(x0), axis=(0, 2), keepdims=True) / 448.0).astype(np.float32)
    out = {}
    for k, v in d.items():
        if k == 'v':
            out['v_bytes'] = e4m3fn_bytes(x0 / s.astype(np.float64))
            out['v_scale'] = s
        else:
            out[k] = v
    return out


def reference(q, k, v_bytes, v_scale, g_v, w_phi, state, g_s):
    return core(q, k, e4m3fn_values(v_bytes) * v_scale.astype(np.float64), g_v, w_phi, state, g_s)

@@ -1,0 +1,337 @@
+import math
+from contextlib import ExitStack
+
+import concourse.mybir as mybir
+from concourse.masks import make_identity
+
+H, N, T, D, R, DV = 2, 512, 1024, 512, 512, 512
+FLOPS = 2 * H * N * (T * D + D * R + T * DV + R * DV)
+
+F32 = mybir.dt.float32
+BF16 = mybir.dt.bfloat16
+U32 = mybir.dt.uint32
+U8 = mybir.dt.uint8
+FP8 = mybir.dt.float8_e4m3fn
+FP8X4 = mybir.dt.float8_e4m3fn_x4
+ACT = mybir.ActivationFunctionType
+ALU = mybir.AluOpType
+
+P = 128
+PACK = 4
+K_PASS = P * PACK
+HALF = K_PASS // 2
+BLOCKS = N // P
+SLABS = 3
+UNITS = H * SLABS * BLOCKS
+ROUNDS = UNITS // 2
+MIX_LAG = 3
+
+
+def tile_lessevictedstatesynthesisattention_kernel(tc, q, k, v_bytes, v_scale, g_v, w_phi, state, g_s, out):
+    nc = tc.nc
+    with ExitStack() as ctx:
+        sb = ctx.enter_context(tc.tile_pool(name="sb", bufs=1))
+        ps = ctx.enter_context(tc.psum_pool(name="ps", bufs=1))
+        ctx.enter_context(tc.manual_schedule())
+
+        def sbuf(name, shape, dtype):
+            return sb.tile(shape, dtype, name=name, align_bytes=64)
+
+        def operand(name):
+            return (sbuf(name + "_codes", [P, K_PASS], U32), sbuf(name + "_scales", [P, K_PASS], U8))
+
+        score_banks = [ps.tile([P, K_PASS], F32, name="score%d" % i) for i in range(2)]
+        turn_banks = [ps.tile([P, K_PASS], F32, name="turn%d" % i) for i in range(2)]
+        row_banks = [ps.tile([P, K_PASS], F32, name="row%d" % i) for i in range(2)]
+        sum_banks = [ps.tile([P, K_PASS], F32, name="sum%d" % i) for i in range(2)]
+        num_banks = [sum_banks + sum_banks, row_banks + sum_banks]
+
+        q_mx = [operand("q%d" % h) for h in range(H)]
+        key_mx = [[operand("key%d_%d" % (h, s)) for s in range(SLABS)] for h in range(H)]
+        value_mx = [[operand("value%d_%d" % (h, s)) for s in range(SLABS)] for h in range(H)]
+
+        def load(name, source, dtype):
+            rows = sbuf(name, list(source.shape), dtype)
+            nc.sync.dma_start(out=rows[:], in_=source)
+            return rows
+
+        def four_rows(matrix):
+            return matrix.rearrange("(p j) c -> p j c", j=PACK)
+
+        turn_jobs = []
+        plain = {}
+        raw = {}
+
+        def load_turned(name, matrix, target, pairs=(0, 1)):
+            for pair in pairs:
+                rows = load("%s_rows%d" % (name, pair), four_rows(matrix)[:, 2 * pair : 2 * pair + 2, :], BF16)
+                turn_jobs.append((rows, target, pair))
+
+        def load_keys(h, g):
+            load_turned("k%d_%d" % (h, g), k[h, g * K_PASS : (g + 1) * K_PASS, :], key_mx[h][1 + g])
+
+        def load_bytes(h, g):
+            raw[h, g] = load("v_bytes%d_%d" % (h, g), four_rows(v_bytes[h, g * K_PASS : (g + 1) * K_PASS, :]), U8)
+
+        plain["w", 0] = load("w0", four_rows(w_phi[0]), BF16)
+        load_turned("q0", q[0], q_mx[0], (0,))
+        load_keys(0, 0)
+        plain["state", 0] = load("state0", four_rows(state[0]), BF16)
+        v_gain = load("v_gain", v_scale.rearrange("a (g p j) b -> p (a g) (j b)", p=P, j=PACK), F32)
+        load_bytes(0, 0)
+        load_keys(0, 1)
+        s_gain = load("s_gain", g_s.rearrange("h (p j) -> p h j", j=PACK), BF16)
+        t_gain = load("t_gain", g_v.rearrange("h (g p j) -> p (h g) j", p=P, j=PACK), BF16)
+        load_turned("q0", q[0], q_mx[0], (1,))
+        load_bytes(0, 1)
+        load_turned("q1", q[1], q_mx[1])
+        plain["w", 1] = load("w1", four_rows(w_phi[1]), BF16)
+        load_keys(1, 0)
+        plain["state", 1] = load("state1", four_rows(state[1]), BF16)
+        load_bytes(1, 0)
+        load_keys(1, 1)
+        load_bytes(1, 1)
+
+        identity = sbuf("identity", [P, P], F32)
+        make_identity(nc, identity[:])
+        mean_weights = sbuf("mean_weights", [P, SLABS * 2], F32)
+        nc.vector.memset(mean_weights[:, :2], 1.0 / R)
+        nc.vector.memset(mean_weights[:, 2:], 1.0 / T)
+
+        def quantize(target, columns, grouped):
+            codes, scales = target
+            nc.vector.quantize_mx(out=codes[:, columns].bitcast(FP8X4), scales=scales[:, columns], in_=grouped)
+
+        turned = [sbuf("turned%d" % i, [P, HALF * PACK], BF16) for i in range(len(turn_jobs))]
+
+        def turn_rows(job, bank):
+            rows = turn_jobs[job][0]
+            for slot in range(2):
+                words = rows[:, slot, :].bitcast(F32)
+                for u in range(2):
+                    first = (2 * slot + u) * P
+                    nc.tensor.transpose(bank[:, first : first + P], words[:, u : 2 * P : 2], identity[:])
+
+        def empty_turned(job, bank):
+            nc.scalar.copy(
+                out=turned[job][:].bitcast(F32).rearrange("p (s m u) -> p s m u", s=2, u=2),
+                in_=bank[:].rearrange("p (s u m) -> p s m u", s=2, u=2),
+            )
+
+        def quantize_turned(job):
+            rows, target, pair = turn_jobs[job]
+            quantize(target, slice(pair * HALF, (pair + 1) * HALF), turned[job][:])
+
+        halves = []
+        widen_jobs = []
+
+        def plain_halves(name, h, target):
+            for c in range(2):
+                halves.append((plain[name, h][:, :, c * HALF : (c + 1) * HALF], target, c))
+
+        def value_halves(h, g):
+            for c in range(2):
+                wide = sbuf("v_wide%d_%d_%d" % (h, g, c), [P, PACK, HALF], BF16)
+                widen_jobs.append((len(halves), wide, h, g, c))
+                halves.append((wide[:], value_mx[h][1 + g], c))
+
+        plain_halves("w", 0, key_mx[0][0])
+        plain_halves("state", 0, value_mx[0][0])
+        value_halves(0, 0)
+        value_halves(0, 1)
+        plain_halves("w", 1, key_mx[1][0])
+        plain_halves("state", 1, value_mx[1][0])
+        value_halves(1, 0)
+        value_halves(1, 1)
+        grouped = [sbuf("grouped%d" % i, [P, HALF * PACK], BF16) for i in range(len(halves))]
+
+        def widen(job):
+            index, wide, h, g, c = job
+            for j in range(PACK):
+                nc.scalar.activation(
+                    out=wide[:, j, :],
+                    in_=raw[h, g][:, j, c * HALF : (c + 1) * HALF].bitcast(FP8),
+                    func=ACT.Copy,
+                    scale=v_gain[:, g, j : j + 1],
+                )
+
+        def interleave(index):
+            nc.vector.tensor_copy(
+                out=grouped[index][:].rearrange("p (c i j) -> p c j i", i=4, j=PACK),
+                in_=halves[index][0].rearrange("p j (c i) -> p c j i", i=4),
+            )
+
+        def quantize_half(index):
+            source, target, c = halves[index]
+            quantize(target, slice(c * HALF, (c + 1) * HALF), grouped[index][:])
+
+        weights = [sbuf("weights%d" % i, [P, K_PASS], F32) for i in range(6)]
+        gained = [sbuf("gained%d" % i, [P, K_PASS], BF16) for i in range(4)]
+        gained_mx = [operand("gained_mx%d" % i) for i in range(H * SLABS)]
+        row_sums = [sbuf("row_sums%d" % i, [P, SLABS * 2], F32) for i in range(2 * H)]
+        row_means = [sbuf("row_means%d" % i, [P, SLABS * 2], F32) for i in range(2 * H)]
+        den = [sbuf("den%d" % i, [P, 2], F32) for i in range(2 * H)]
+        inv_den = [sbuf("inv_den%d" % i, [P, 2], F32) for i in range(2 * H)]
+
+        round_plan = [(0, s, pair) for pair in range(2) for s in range(SLABS)]
+        round_plan = round_plan + [(1, s, pair) for s in range(SLABS) for pair in range(2)]
+
+        def place(unit):
+            h, s, pair = round_plan[unit // 2]
+            return h, s, 2 * pair + unit % 2
+
+        def matmul(bank, left, columns, right, start, stop):
+            nc.tensor.matmul_mx(
+                out=bank[:],
+                lhsT=left[0][:, columns].bitcast(FP8X4),
+                lhsT_scale=left[1][:, columns],
+                rhs=right[0][:].bitcast(FP8X4),
+                rhs_scale=right[1][:],
+                start=start,
+                stop=stop,
+            )
+
+        def scores(unit):
+            h, s, b = place(unit)
+            matmul(score_banks[unit % 2], q_mx[h], slice(b * P, (b + 1) * P), key_mx[h][s], True, True)
+
+        def weigh(unit):
+            h, s, b = place(unit)
+            bank = score_banks[unit % 2]
+            target = weights[unit % len(weights)]
+            total = row_sums[2 * h + b // 2][:, 2 * s + b % 2 : 2 * s + b % 2 + 1]
+            if s == 0:
+                nc.scalar.activation(
+                    out=target[:].rearrange("p (j m) -> p j m", j=PACK),
+                    in_=bank[:].rearrange("p (m j) -> p j m", j=PACK),
+                    func=ACT.Abs,
+                    accum_out=total,
+                )
+            else:
+                nc.scalar.activation(out=target[:], in_=bank[:], func=ACT.Exp, scale=1.0 / math.sqrt(D), accum_out=total)
+
+        def turn_weights(unit):
+            source = weights[unit % len(weights)]
+            bank = turn_banks[unit % 2]
+            for j in range(PACK):
+                nc.tensor.transpose(bank[:, j * P : (j + 1) * P], source[:, j * P : (j + 1) * P], identity[:])
+
+        def apply_gain(unit):
+            h, s, b = place(unit)
+            gain = s_gain[:, h, :] if s == 0 else t_gain[:, 2 * h + s - 1, :]
+            nc.vector.tensor_tensor(
+                out=gained[unit % len(gained)][:].rearrange("p (n j) -> p n j", j=PACK),
+                in0=turn_banks[unit % 2][:].rearrange("p (j n) -> p n j", j=PACK),
+                in1=gain.unsqueeze(1).to_broadcast([P, P, PACK]),
+                op=ALU.mult,
+            )
+
+        def quantize_gained(unit):
+            h, s, b = place(unit)
+            quantize(gained_mx[h * SLABS + s], slice(b * P, (b + 1) * P), gained[unit % len(gained)][:])
+
+        def mix(unit):
+            h, s, b = place(unit)
+            matmul(num_banks[h][b], gained_mx[h * SLABS + s], slice(b * P, (b + 1) * P), value_mx[h][s], s == 0, s == SLABS - 1)
+
+        def divide_and_store(unit):
+            h, s, b = place(unit)
+            result = sbuf("result%d_%d" % (h, b), [P, DV], F32)
+            factor = inv_den[2 * h + b // 2][:, b % 2 : b % 2 + 1]
+            if unit == UNITS - 1:
+                nc.vector.tensor_scalar(out=result[:], in0=num_banks[h][b][:], scalar1=factor, scalar2=None, op0=ALU.mult)
+            else:
+                nc.scalar.activation(out=result[:], in_=num_banks[h][b][:], func=ACT.Copy, scale=factor)
+            nc.sync.dma_start(out=four_rows(out[h])[:, b, :], in_=result[:])
+
+        def means(h):
+            nc.vector.tensor_tensor(out=row_means[h][:], in0=row_sums[h][:], in1=mean_weights[:], op=ALU.mult)
+
+        def add_means(h):
+            nc.vector.tensor_reduce(
+                out=den[h][:], in_=row_means[h][:].rearrange("p (s b) -> p b s", s=SLABS), axis=mybir.AxisListType.X, op=ALU.add
+            )
+
+        def invert(h):
+            nc.vector.reciprocal(out=inv_den[h][:], in_=den[h][:])
+
+        def units_of(r):
+            return [u for u in (2 * r, 2 * r + 1) if 0 <= u < UNITS]
+
+        def last_slab(units):
+            return [u for u in units if place(u)[1] == SLABS - 1]
+
+        def job_bank(job):
+            return (row_banks + sum_banks)[job] if job < 4 else row_banks[job % 2]
+
+        last_round = ROUNDS + MIX_LAG
+        jobs_in = {r: [r + 4] for r in range(1, len(turn_jobs) - 4)}
+        jobs_in[-1] = [1, 2]
+        jobs_in[0] = [3, 4]
+        halves_in = {0: [2, 3], 5: [8, 9]}
+        for r in range(1, 5):
+            halves_in[r] = [r + 3]
+        for r in range(6, 12):
+            halves_in[r] = [r + 4]
+        store_rounds = [r for r in range(last_round) if last_slab(units_of(r - MIX_LAG))]
+        widen_round = {}
+        for job in reversed(widen_jobs):
+            r = min(i for i in halves_in if job[0] in halves_in[i]) - 1
+            while r in store_rounds or r in widen_round:
+                r = r - 1
+            widen_round[r] = job
+
+        for job in range(3):
+            turn_rows(job, job_bank(job))
+            empty_turned(job, job_bank(job))
+        interleave(0)
+        interleave(1)
+        quantize_half(0)
+        quantize_half(1)
+        quantize_turned(0)
+
+        for r in range(last_round):
+            finished = last_slab(units_of(r - 1))
+            pair = 2 * place(finished[0])[0] + place(finished[0])[2] // 2 if finished else None
+
+            turning = jobs_in.get(r, [])
+            for u in units_of(r):
+                scores(u)
+            if not turning:
+                for u in units_of(r - MIX_LAG):
+                    mix(u)
+            for u in units_of(r):
+                weigh(u)
+            for u in units_of(r - 1):
+                turn_weights(u)
+            if turning:
+                for u in units_of(r - MIX_LAG):
+                    mix(u)
+            for job in turning:
+                turn_rows(job, job_bank(job))
+            for u in last_slab(units_of(r - MIX_LAG)):
+                divide_and_store(u)
+            if r in widen_round:
+                widen(widen_round[r])
+
+            for half in halves_in.get(r, []):
+                interleave(half)
+            if finished:
+                means(pair)
+            for job in jobs_in.get(r - 1, []):
+                quantize_turned(job)
+            for u in units_of(r - 1)[:1]:
+                apply_gain(u)
+            if finished:
+                add_means(pair)
+            for u in units_of(r - 1)[1:]:
+                apply_gain(u)
+            for half in halves_in.get(r, []):
+                quantize_half(half)
+            if finished:
+                invert(pair)
+            for u in units_of(r - 1):
+                quantize_gained(u)
+
+            for job in turning:
+                empty_turned(job, job_bank(job))

@@ -74,18 +74,18 @@ def tile_lessevictedstatesynthesisattention_kernel(tc, q, k, v_bytes, v_scale, g
             raw[h, g] = load("v_bytes%d_%d" % (h, g), four_rows(v_bytes[h, g * K_PASS : (g + 1) * K_PASS, :]), U8)
 
         plain["w", 0] = load("w0", four_rows(w_phi[0]), BF16)
+        v_gain = load("v_gain", v_scale.rearrange("a (g p j) b -> p (a g) (j b)", p=P, j=PACK), F32)
+        load_bytes(0, 0)
         load_turned("q0", q[0], q_mx[0], (0,))
         load_keys(0, 0)
         plain["state", 0] = load("state0", four_rows(state[0]), BF16)
-        v_gain = load("v_gain", v_scale.rearrange("a (g p j) b -> p (a g) (j b)", p=P, j=PACK), F32)
-        load_bytes(0, 0)
         load_keys(0, 1)
+        load_bytes(0, 1)
         s_gain = load("s_gain", g_s.rearrange("h (p j) -> p h j", j=PACK), BF16)
         t_gain = load("t_gain", g_v.rearrange("h (g p j) -> p (h g) j", p=P, j=PACK), BF16)
         load_turned("q0", q[0], q_mx[0], (1,))
-        load_bytes(0, 1)
-        load_turned("q1", q[1], q_mx[1])
         plain["w", 1] = load("w1", four_rows(w_phi[1]), BF16)
+        load_turned("q1", q[1], q_mx[1])
         load_keys(1, 0)
         plain["state", 1] = load("state1", four_rows(state[1]), BF16)
         load_bytes(1, 0)
@@ -136,8 +136,8 @@ def tile_lessevictedstatesynthesisattention_kernel(tc, q, k, v_bytes, v_scale, g
                 halves.append((wide[:], value_mx[h][1 + g], c))
 
         plain_halves("w", 0, key_mx[0][0])
-        plain_halves("state", 0, value_mx[0][0])
         value_halves(0, 0)
+        plain_halves("state", 0, value_mx[0][0])
         value_halves(0, 1)
         plain_halves("w", 1, key_mx[1][0])
         plain_halves("state", 1, value_mx[1][0])
@@ -239,10 +239,13 @@ def tile_lessevictedstatesynthesisattention_kernel(tc, q, k, v_bytes, v_scale, g
             result = sbuf("result%d_%d" % (h, b), [P, DV], F32)
             factor = inv_den[2 * h + b // 2][:, b % 2 : b % 2 + 1]
             if unit == UNITS - 1:
-                nc.vector.tensor_scalar(out=result[:], in0=num_banks[h][b][:], scalar1=factor, scalar2=None, op0=ALU.mult)
+                for c in range(2):
+                    columns = slice(c * HALF, (c + 1) * HALF)
+                    nc.vector.tensor_scalar(out=result[:, columns], in0=num_banks[h][b][:, columns], scalar1=factor, scalar2=None, op0=ALU.mult)
+                    nc.sync.dma_start(out=four_rows(out[h])[:, b, columns], in_=result[:, columns])
             else:
                 nc.scalar.activation(out=result[:], in_=num_banks[h][b][:], func=ACT.Copy, scale=factor)
-            nc.sync.dma_start(out=four_rows(out[h])[:, b, :], in_=result[:])
+                nc.sync.dma_start(out=four_rows(out[h])[:, b, :], in_=result[:])
 
         def means(h):
             nc.vector.tensor_tensor(out=row_means[h][:], in0=row_sums[h][:], in1=mean_weights[:], op=ALU.mult)
@@ -268,27 +271,37 @@ def tile_lessevictedstatesynthesisattention_kernel(tc, q, k, v_bytes, v_scale, g
         jobs_in = {r: [r + 4] for r in range(1, len(turn_jobs) - 4)}
         jobs_in[-1] = [1, 2]
         jobs_in[0] = [3, 4]
-        halves_in = {0: [2, 3], 5: [8, 9]}
-        for r in range(1, 5):
-            halves_in[r] = [r + 3]
-        for r in range(6, 12):
-            halves_in[r] = [r + 4]
+        halves_in = {-1: [3], 0: [4, 5]}
+        for r in range(1, 11):
+            halves_in[r] = [r + 5]
         store_rounds = [r for r in range(last_round) if last_slab(units_of(r - MIX_LAG))]
         widen_round = {}
-        for job in reversed(widen_jobs):
+        for job in reversed(widen_jobs[2:]):
             r = min(i for i in halves_in if job[0] in halves_in[i]) - 1
             while r in store_rounds or r in widen_round:
                 r = r - 1
             widen_round[r] = job
 
+        def keep_clock(count, bank):
+            for i in range(count):
+                nc.tensor.matmul(bank[:, :P], lhsT=identity[:], rhs=identity[:], start=True, stop=True)
+
+        keep_clock(8, turn_banks[0])
         for job in range(3):
             turn_rows(job, job_bank(job))
+            if job < 2:
+                keep_clock(2, turn_banks[0])
+            if job < 2:
+                widen(widen_jobs[job])
             empty_turned(job, job_bank(job))
         interleave(0)
         interleave(1)
         quantize_half(0)
         quantize_half(1)
+        interleave(2)
         quantize_turned(0)
+        interleave(3)
+        quantize_half(2)
 
         for r in range(last_round):
             finished = last_slab(units_of(r - 1))
@@ -307,15 +320,19 @@ def tile_lessevictedstatesynthesisattention_kernel(tc, q, k, v_bytes, v_scale, g
             if turning:
                 for u in units_of(r - MIX_LAG):
                     mix(u)
+            if 0 < r < MIX_LAG:
+                keep_clock(2, sum_banks[0])
             for job in turning:
                 turn_rows(job, job_bank(job))
+                if job == 3:
+                    keep_clock(2, turn_banks[0])
             for u in last_slab(units_of(r - MIX_LAG)):
                 divide_and_store(u)
             if r in widen_round:
                 widen(widen_round[r])
 
-            for half in halves_in.get(r, []):
-                interleave(half)
+            for half in halves_in.get(r - 1, []):
+                quantize_half(half)
             if finished:
                 means(pair)
             for job in jobs_in.get(r - 1, []):
@@ -324,14 +341,17 @@ def tile_lessevictedstatesynthesisattention_kernel(tc, q, k, v_bytes, v_scale, g
                 apply_gain(u)
             if finished:
                 add_means(pair)
+            if r == ROUNDS:
+                quantize_gained(UNITS - 2)
             for u in units_of(r - 1)[1:]:
                 apply_gain(u)
             for half in halves_in.get(r, []):
-                quantize_half(half)
+                interleave(half)
             if finished:
                 invert(pair)
             for u in units_of(r - 1):
-                quantize_gained(u)
+                if u != UNITS - 2:
+                    quantize_gained(u)
 
             for job in turning:
                 empty_turned(job, job_bank(job))

@@ -25,6 +25,9 @@ SLABS = 3
 UNITS = H * SLABS * BLOCKS
 ROUNDS = UNITS // 2
 MIX_LAG = 3
+ON_VECTOR = (3, 6, 13)
+SHARED_FROM = 6
+POOL_COLUMNS = 128
 
 
 def tile_lessevictedstatesynthesisattention_kernel(tc, q, k, v_bytes, v_scale, g_v, w_phi, state, g_s, out):
@@ -95,8 +98,8 @@ def tile_lessevictedstatesynthesisattention_kernel(tc, q, k, v_bytes, v_scale, g
         identity = sbuf("identity", [P, P], F32)
         make_identity(nc, identity[:])
         mean_weights = sbuf("mean_weights", [P, SLABS * 2], F32)
-        nc.vector.memset(mean_weights[:, :2], 1.0 / R)
         nc.vector.memset(mean_weights[:, 2:], 1.0 / T)
+        nc.scalar.activation(out=mean_weights[:, :2], in_=mean_weights[:, 2:4], func=ACT.Copy, scale=float(T // R))
 
         def quantize(target, columns, grouped):
             codes, scales = target
@@ -143,22 +146,34 @@ def tile_lessevictedstatesynthesisattention_kernel(tc, q, k, v_bytes, v_scale, g
         plain_halves("state", 1, value_mx[1][0])
         value_halves(1, 0)
         value_halves(1, 1)
-        grouped = [sbuf("grouped%d" % i, [P, HALF * PACK], BF16) for i in range(len(halves))]
+        grouped = [sbuf("grouped%d" % i, [P, HALF * PACK], BF16) for i in range(SHARED_FROM)]
+        grouped = grouped + [grouped[SHARED_FROM - 1]] * (len(halves) - SHARED_FROM)
 
         def widen(job):
             index, wide, h, g, c = job
             for j in range(PACK):
-                nc.scalar.activation(
-                    out=wide[:, j, :],
-                    in_=raw[h, g][:, j, c * HALF : (c + 1) * HALF].bitcast(FP8),
-                    func=ACT.Copy,
-                    scale=v_gain[:, g, j : j + 1],
-                )
+                codes = raw[h, g][:, j, c * HALF : (c + 1) * HALF].bitcast(FP8)
+                factor = v_gain[:, g, j : j + 1]
+                if index in ON_VECTOR:
+                    nc.vector.tensor_scalar(out=wide[:, j, :], in0=codes, scalar1=factor, scalar2=None, op0=ALU.mult)
+                else:
+                    nc.scalar.activation(out=wide[:, j, :], in_=codes, func=ACT.Copy, scale=factor)
 
         def interleave(index):
+            first = POOL_COLUMNS if index >= SHARED_FROM else 0
             nc.vector.tensor_copy(
-                out=grouped[index][:].rearrange("p (c i j) -> p c j i", i=4, j=PACK),
-                in_=halves[index][0].rearrange("p j (c i) -> p c j i", i=4),
+                out=grouped[index][:, first * PACK :].rearrange("p (c i j) -> p c j i", i=4, j=PACK),
+                in_=halves[index][0][:, :, first:].rearrange("p j (c i) -> p c j i", i=4),
+            )
+
+        def interleave_aside(index):
+            nc.gpsimd.tensor_scalar(
+                out=grouped[index][:, : POOL_COLUMNS * PACK].rearrange("p (c j) -> p c j", j=PACK),
+                in0=halves[index][0][:, :, :POOL_COLUMNS].rearrange("p j c -> p c j"),
+                scalar1=1.0,
+                scalar2=0.0,
+                op0=ALU.mult,
+                op1=ALU.add,
             )
 
         def quantize_half(index):
@@ -166,7 +181,7 @@ def tile_lessevictedstatesynthesisattention_kernel(tc, q, k, v_bytes, v_scale, g
             quantize(target, slice(c * HALF, (c + 1) * HALF), grouped[index][:])
 
         weights = [sbuf("weights%d" % i, [P, K_PASS], F32) for i in range(6)]
-        gained = [sbuf("gained%d" % i, [P, K_PASS], BF16) for i in range(4)]
+        gained = [sbuf("gained%d" % i, [P, 2, K_PASS], BF16) for i in range(2)]
         gained_mx = [operand("gained_mx%d" % i) for i in range(H * SLABS)]
         row_sums = [sbuf("row_sums%d" % i, [P, SLABS * 2], F32) for i in range(2 * H)]
         row_means = [sbuf("row_means%d" % i, [P, SLABS * 2], F32) for i in range(2 * H)]
@@ -220,15 +235,17 @@ def tile_lessevictedstatesynthesisattention_kernel(tc, q, k, v_bytes, v_scale, g
             h, s, b = place(unit)
             gain = s_gain[:, h, :] if s == 0 else t_gain[:, 2 * h + s - 1, :]
             nc.vector.tensor_tensor(
-                out=gained[unit % len(gained)][:].rearrange("p (n j) -> p n j", j=PACK),
+                out=gained[unit // 2 % 2][:, unit % 2, :].rearrange("p (n j) -> p n j", j=PACK),
                 in0=turn_banks[unit % 2][:].rearrange("p (j n) -> p n j", j=PACK),
                 in1=gain.unsqueeze(1).to_broadcast([P, P, PACK]),
                 op=ALU.mult,
             )
 
-        def quantize_gained(unit):
-            h, s, b = place(unit)
-            quantize(gained_mx[h * SLABS + s], slice(b * P, (b + 1) * P), gained[unit % len(gained)][:])
+        def quantize_gained(units):
+            h, s, b = place(units[0])
+            first = units[0] % 2
+            source = gained[units[0] // 2 % 2][:, first : first + len(units), :].rearrange("p u c -> p (u c)")
+            quantize(gained_mx[h * SLABS + s], slice(b * P, (b + len(units)) * P), source)
 
         def mix(unit):
             h, s, b = place(unit)
@@ -291,8 +308,8 @@ def tile_lessevictedstatesynthesisattention_kernel(tc, q, k, v_bytes, v_scale, g
             turn_rows(job, job_bank(job))
             if job < 2:
                 keep_clock(2, turn_banks[0])
-            if job < 2:
-                widen(widen_jobs[job])
+            if job == 0:
+                widen(widen_jobs[0])
             empty_turned(job, job_bank(job))
         interleave(0)
         interleave(1)
@@ -300,8 +317,9 @@ def tile_lessevictedstatesynthesisattention_kernel(tc, q, k, v_bytes, v_scale, g
         quantize_half(1)
         interleave(2)
         quantize_turned(0)
-        interleave(3)
+        widen(widen_jobs[1])
         quantize_half(2)
+        interleave(3)
 
         for r in range(last_round):
             finished = last_slab(units_of(r - 1))
@@ -310,18 +328,14 @@ def tile_lessevictedstatesynthesisattention_kernel(tc, q, k, v_bytes, v_scale, g
             turning = jobs_in.get(r, [])
             for u in units_of(r):
                 scores(u)
-            if not turning:
-                for u in units_of(r - MIX_LAG):
-                    mix(u)
+            for u in units_of(r - MIX_LAG):
+                mix(u)
+            if 0 < r < MIX_LAG:
+                keep_clock(2, sum_banks[0])
             for u in units_of(r):
                 weigh(u)
             for u in units_of(r - 1):
                 turn_weights(u)
-            if turning:
-                for u in units_of(r - MIX_LAG):
-                    mix(u)
-            if 0 < r < MIX_LAG:
-                keep_clock(2, sum_banks[0])
             for job in turning:
                 turn_rows(job, job_bank(job))
                 if job == 3:
@@ -331,27 +345,33 @@ def tile_lessevictedstatesynthesisattention_kernel(tc, q, k, v_bytes, v_scale, g
             if r in widen_round:
                 widen(widen_round[r])
 
+            for job in jobs_in.get(r - 1, []):
+                if job < 6:
+                    quantize_turned(job)
+            for job in jobs_in.get(r - 2, []):
+                if job >= 6:
+                    quantize_turned(job)
             for half in halves_in.get(r - 1, []):
                 quantize_half(half)
+            for half in halves_in.get(r, []):
+                if half >= SHARED_FROM:
+                    interleave_aside(half)
             if finished:
                 means(pair)
-            for job in jobs_in.get(r - 1, []):
-                quantize_turned(job)
             for u in units_of(r - 1)[:1]:
                 apply_gain(u)
             if finished:
                 add_means(pair)
             if r == ROUNDS:
-                quantize_gained(UNITS - 2)
+                quantize_gained([UNITS - 2])
             for u in units_of(r - 1)[1:]:
                 apply_gain(u)
             for half in halves_in.get(r, []):
                 interleave(half)
             if finished:
                 invert(pair)
-            for u in units_of(r - 1):
-                if u != UNITS - 2:
-                    quantize_gained(u)
+            if 1 <= r <= ROUNDS:
+                quantize_gained([u for u in units_of(r - 1) if u != UNITS - 2])
 
             for job in turning:
                 empty_turned(job, job_bank(job))

@@ -25,9 +25,9 @@ SLABS = 3
 UNITS = H * SLABS * BLOCKS
 ROUNDS = UNITS // 2
 MIX_LAG = 3
-ON_VECTOR = (3, 6, 13)
+ON_VECTOR = (3, 7, 13)
 SHARED_FROM = 6
-POOL_COLUMNS = 128
+POOL_COLUMNS = 160
 
 
 def tile_lessevictedstatesynthesisattention_kernel(tc, q, k, v_bytes, v_scale, g_v, w_phi, state, g_s, out):
@@ -76,9 +76,9 @@ def tile_lessevictedstatesynthesisattention_kernel(tc, q, k, v_bytes, v_scale, g
         def load_bytes(h, g):
             raw[h, g] = load("v_bytes%d_%d" % (h, g), four_rows(v_bytes[h, g * K_PASS : (g + 1) * K_PASS, :]), U8)
 
-        plain["w", 0] = load("w0", four_rows(w_phi[0]), BF16)
         v_gain = load("v_gain", v_scale.rearrange("a (g p j) b -> p (a g) (j b)", p=P, j=PACK), F32)
         load_bytes(0, 0)
+        plain["w", 0] = load("w0", four_rows(w_phi[0]), BF16)
         load_turned("q0", q[0], q_mx[0], (0,))
         load_keys(0, 0)
         plain["state", 0] = load("state0", four_rows(state[0]), BF16)
@@ -288,7 +288,7 @@ def tile_lessevictedstatesynthesisattention_kernel(tc, q, k, v_bytes, v_scale, g
         jobs_in = {r: [r + 4] for r in range(1, len(turn_jobs) - 4)}
         jobs_in[-1] = [1, 2]
         jobs_in[0] = [3, 4]
-        halves_in = {-1: [3], 0: [4, 5]}
+        halves_in = {-1: [2], 0: [4, 5]}
         for r in range(1, 11):
             halves_in[r] = [r + 5]
         store_rounds = [r for r in range(last_round) if last_slab(units_of(r - MIX_LAG))]
@@ -306,20 +306,20 @@ def tile_lessevictedstatesynthesisattention_kernel(tc, q, k, v_bytes, v_scale, g
         keep_clock(8, turn_banks[0])
         for job in range(3):
             turn_rows(job, job_bank(job))
-            if job < 2:
+            if job == 0:
                 keep_clock(2, turn_banks[0])
             if job == 0:
                 widen(widen_jobs[0])
             empty_turned(job, job_bank(job))
+        widen(widen_jobs[1])
+        interleave(3)
         interleave(0)
         interleave(1)
         quantize_half(0)
         quantize_half(1)
-        interleave(2)
         quantize_turned(0)
-        widen(widen_jobs[1])
-        quantize_half(2)
-        interleave(3)
+        interleave(2)
+        quantize_half(3)
 
         for r in range(last_round):
             finished = last_slab(units_of(r - 1))

import math
from contextlib import ExitStack

import concourse.mybir as mybir
from concourse.masks import make_identity

H, N, T, D, R, DV = 2, 512, 1024, 512, 512, 512
FLOPS = 2 * H * N * (T * D + D * R + T * DV + R * DV)

F32 = mybir.dt.float32
BF16 = mybir.dt.bfloat16
U32 = mybir.dt.uint32
U8 = mybir.dt.uint8
FP8 = mybir.dt.float8_e4m3fn
FP8X4 = mybir.dt.float8_e4m3fn_x4
ACT = mybir.ActivationFunctionType
ALU = mybir.AluOpType

P = 128
PACK = 4
K_PASS = P * PACK
HALF = K_PASS // 2
BLOCKS = N // P
SLABS = 3
UNITS = H * SLABS * BLOCKS
ROUNDS = UNITS // 2
MIX_LAG = 3
ON_VECTOR = (3, 7, 13)
SHARED_FROM = 6
POOL_COLUMNS = 160


def tile_lessevictedstatesynthesisattention_kernel(tc, q, k, v_bytes, v_scale, g_v, w_phi, state, g_s, out):
    nc = tc.nc
    with ExitStack() as ctx:
        sb = ctx.enter_context(tc.tile_pool(name="sb", bufs=1))
        ps = ctx.enter_context(tc.psum_pool(name="ps", bufs=1))
        ctx.enter_context(tc.manual_schedule())

        def sbuf(name, shape, dtype):
            return sb.tile(shape, dtype, name=name, align_bytes=64)

        def operand(name):
            return (sbuf(name + "_codes", [P, K_PASS], U32), sbuf(name + "_scales", [P, K_PASS], U8))

        score_banks = [ps.tile([P, K_PASS], F32, name="score%d" % i) for i in range(2)]
        turn_banks = [ps.tile([P, K_PASS], F32, name="turn%d" % i) for i in range(2)]
        row_banks = [ps.tile([P, K_PASS], F32, name="row%d" % i) for i in range(2)]
        sum_banks = [ps.tile([P, K_PASS], F32, name="sum%d" % i) for i in range(2)]
        num_banks = [sum_banks + sum_banks, row_banks + sum_banks]

        q_mx = [operand("q%d" % h) for h in range(H)]
        key_mx = [[operand("key%d_%d" % (h, s)) for s in range(SLABS)] for h in range(H)]
        value_mx = [[operand("value%d_%d" % (h, s)) for s in range(SLABS)] for h in range(H)]

        def load(name, source, dtype):
            rows = sbuf(name, list(source.shape), dtype)
            nc.sync.dma_start(out=rows[:], in_=source)
            return rows

        def four_rows(matrix):
            return matrix.rearrange("(p j) c -> p j c", j=PACK)

        turn_jobs = []
        plain = {}
        raw = {}

        def load_turned(name, matrix, target, pairs=(0, 1)):
            for pair in pairs:
                rows = load("%s_rows%d" % (name, pair), four_rows(matrix)[:, 2 * pair : 2 * pair + 2, :], BF16)
                turn_jobs.append((rows, target, pair))

        def load_keys(h, g):
            load_turned("k%d_%d" % (h, g), k[h, g * K_PASS : (g + 1) * K_PASS, :], key_mx[h][1 + g])

        def load_bytes(h, g):
            raw[h, g] = load("v_bytes%d_%d" % (h, g), four_rows(v_bytes[h, g * K_PASS : (g + 1) * K_PASS, :]), U8)

        v_gain = load("v_gain", v_scale.rearrange("a (g p j) b -> p (a g) (j b)", p=P, j=PACK), F32)
        load_bytes(0, 0)
        plain["w", 0] = load("w0", four_rows(w_phi[0]), BF16)
        load_turned("q0", q[0], q_mx[0], (0,))
        load_keys(0, 0)
        plain["state", 0] = load("state0", four_rows(state[0]), BF16)
        load_keys(0, 1)
        load_bytes(0, 1)
        s_gain = load("s_gain", g_s.rearrange("h (p j) -> p h j", j=PACK), BF16)
        t_gain = load("t_gain", g_v.rearrange("h (g p j) -> p (h g) j", p=P, j=PACK), BF16)
        load_turned("q0", q[0], q_mx[0], (1,))
        plain["w", 1] = load("w1", four_rows(w_phi[1]), BF16)
        load_turned("q1", q[1], q_mx[1])
        load_keys(1, 0)
        plain["state", 1] = load("state1", four_rows(state[1]), BF16)
        load_bytes(1, 0)
        load_keys(1, 1)
        load_bytes(1, 1)

        identity = sbuf("identity", [P, P], F32)
        make_identity(nc, identity[:])
        mean_weights = sbuf("mean_weights", [P, SLABS * 2], F32)
        nc.vector.memset(mean_weights[:, 2:], 1.0 / T)
        nc.scalar.activation(out=mean_weights[:, :2], in_=mean_weights[:, 2:4], func=ACT.Copy, scale=float(T // R))

        def quantize(target, columns, grouped):
            codes, scales = target
            nc.vector.quantize_mx(out=codes[:, columns].bitcast(FP8X4), scales=scales[:, columns], in_=grouped)

        turned = [sbuf("turned%d" % i, [P, HALF * PACK], BF16) for i in range(len(turn_jobs))]

        def turn_rows(job, bank):
            rows = turn_jobs[job][0]
            for slot in range(2):
                words = rows[:, slot, :].bitcast(F32)
                for u in range(2):
                    first = (2 * slot + u) * P
                    nc.tensor.transpose(bank[:, first : first + P], words[:, u : 2 * P : 2], identity[:])

        def empty_turned(job, bank):
            nc.scalar.copy(
                out=turned[job][:].bitcast(F32).rearrange("p (s m u) -> p s m u", s=2, u=2),
                in_=bank[:].rearrange("p (s u m) -> p s m u", s=2, u=2),
            )

        def quantize_turned(job):
            rows, target, pair = turn_jobs[job]
            quantize(target, slice(pair * HALF, (pair + 1) * HALF), turned[job][:])

        halves = []
        widen_jobs = []

        def plain_halves(name, h, target):
            for c in range(2):
                halves.append((plain[name, h][:, :, c * HALF : (c + 1) * HALF], target, c))

        def value_halves(h, g):
            for c in range(2):
                wide = sbuf("v_wide%d_%d_%d" % (h, g, c), [P, PACK, HALF], BF16)
                widen_jobs.append((len(halves), wide, h, g, c))
                halves.append((wide[:], value_mx[h][1 + g], c))

        plain_halves("w", 0, key_mx[0][0])
        value_halves(0, 0)
        plain_halves("state", 0, value_mx[0][0])
        value_halves(0, 1)
        plain_halves("w", 1, key_mx[1][0])
        plain_halves("state", 1, value_mx[1][0])
        value_halves(1, 0)
        value_halves(1, 1)
        grouped = [sbuf("grouped%d" % i, [P, HALF * PACK], BF16) for i in range(SHARED_FROM)]
        grouped = grouped + [grouped[SHARED_FROM - 1]] * (len(halves) - SHARED_FROM)

        def widen(job):
            index, wide, h, g, c = job
            for j in range(PACK):
                codes = raw[h, g][:, j, c * HALF : (c + 1) * HALF].bitcast(FP8)
                factor = v_gain[:, g, j : j + 1]
                if index in ON_VECTOR:
                    nc.vector.tensor_scalar(out=wide[:, j, :], in0=codes, scalar1=factor, scalar2=None, op0=ALU.mult)
                else:
                    nc.scalar.activation(out=wide[:, j, :], in_=codes, func=ACT.Copy, scale=factor)

        def interleave(index):
            first = POOL_COLUMNS if index >= SHARED_FROM else 0
            nc.vector.tensor_copy(
                out=grouped[index][:, first * PACK :].rearrange("p (c i j) -> p c j i", i=4, j=PACK),
                in_=halves[index][0][:, :, first:].rearrange("p j (c i) -> p c j i", i=4),
            )

        def interleave_aside(index):
            nc.gpsimd.tensor_scalar(
                out=grouped[index][:, : POOL_COLUMNS * PACK].rearrange("p (c j) -> p c j", j=PACK),
                in0=halves[index][0][:, :, :POOL_COLUMNS].rearrange("p j c -> p c j"),
                scalar1=1.0,
                scalar2=0.0,
                op0=ALU.mult,
                op1=ALU.add,
            )

        def quantize_half(index):
            source, target, c = halves[index]
            quantize(target, slice(c * HALF, (c + 1) * HALF), grouped[index][:])

        weights = [sbuf("weights%d" % i, [P, K_PASS], F32) for i in range(6)]
        gained = [sbuf("gained%d" % i, [P, 2, K_PASS], BF16) for i in range(2)]
        gained_mx = [operand("gained_mx%d" % i) for i in range(H * SLABS)]
        row_sums = [sbuf("row_sums%d" % i, [P, SLABS * 2], F32) for i in range(2 * H)]
        row_means = [sbuf("row_means%d" % i, [P, SLABS * 2], F32) for i in range(2 * H)]
        den = [sbuf("den%d" % i, [P, 2], F32) for i in range(2 * H)]
        inv_den = [sbuf("inv_den%d" % i, [P, 2], F32) for i in range(2 * H)]

        round_plan = [(0, s, pair) for pair in range(2) for s in range(SLABS)]
        round_plan = round_plan + [(1, s, pair) for s in range(SLABS) for pair in range(2)]

        def place(unit):
            h, s, pair = round_plan[unit // 2]
            return h, s, 2 * pair + unit % 2

        def matmul(bank, left, columns, right, start, stop):
            nc.tensor.matmul_mx(
                out=bank[:],
                lhsT=left[0][:, columns].bitcast(FP8X4),
                lhsT_scale=left[1][:, columns],
                rhs=right[0][:].bitcast(FP8X4),
                rhs_scale=right[1][:],
                start=start,
                stop=stop,
            )

        def scores(unit):
            h, s, b = place(unit)
            matmul(score_banks[unit % 2], q_mx[h], slice(b * P, (b + 1) * P), key_mx[h][s], True, True)

        def weigh(unit):
            h, s, b = place(unit)
            bank = score_banks[unit % 2]
            target = weights[unit % len(weights)]
            total = row_sums[2 * h + b // 2][:, 2 * s + b % 2 : 2 * s + b % 2 + 1]
            if s == 0:
                nc.scalar.activation(
                    out=target[:].rearrange("p (j m) -> p j m", j=PACK),
                    in_=bank[:].rearrange("p (m j) -> p j m", j=PACK),
                    func=ACT.Abs,
                    accum_out=total,
                )
            else:
                nc.scalar.activation(out=target[:], in_=bank[:], func=ACT.Exp, scale=1.0 / math.sqrt(D), accum_out=total)

        def turn_weights(unit):
            source = weights[unit % len(weights)]
            bank = turn_banks[unit % 2]
            for j in range(PACK):
                nc.tensor.transpose(bank[:, j * P : (j + 1) * P], source[:, j * P : (j + 1) * P], identity[:])

        def apply_gain(unit):
            h, s, b = place(unit)
            gain = s_gain[:, h, :] if s == 0 else t_gain[:, 2 * h + s - 1, :]
            nc.vector.tensor_tensor(
                out=gained[unit // 2 % 2][:, unit % 2, :].rearrange("p (n j) -> p n j", j=PACK),
                in0=turn_banks[unit % 2][:].rearrange("p (j n) -> p n j", j=PACK),
                in1=gain.unsqueeze(1).to_broadcast([P, P, PACK]),
                op=ALU.mult,
            )

        def quantize_gained(units):
            h, s, b = place(units[0])
            first = units[0] % 2
            source = gained[units[0] // 2 % 2][:, first : first + len(units), :].rearrange("p u c -> p (u c)")
            quantize(gained_mx[h * SLABS + s], slice(b * P, (b + len(units)) * P), source)

        def mix(unit):
            h, s, b = place(unit)
            matmul(num_banks[h][b], gained_mx[h * SLABS + s], slice(b * P, (b + 1) * P), value_mx[h][s], s == 0, s == SLABS - 1)

        def divide_and_store(unit):
            h, s, b = place(unit)
            result = sbuf("result%d_%d" % (h, b), [P, DV], F32)
            factor = inv_den[2 * h + b // 2][:, b % 2 : b % 2 + 1]
            if unit == UNITS - 1:
                for c in range(2):
                    columns = slice(c * HALF, (c + 1) * HALF)
                    nc.vector.tensor_scalar(out=result[:, columns], in0=num_banks[h][b][:, columns], scalar1=factor, scalar2=None, op0=ALU.mult)
                    nc.sync.dma_start(out=four_rows(out[h])[:, b, columns], in_=result[:, columns])
            else:
                nc.scalar.activation(out=result[:], in_=num_banks[h][b][:], func=ACT.Copy, scale=factor)
                nc.sync.dma_start(out=four_rows(out[h])[:, b, :], in_=result[:])

        def means(h):
            nc.vector.tensor_tensor(out=row_means[h][:], in0=row_sums[h][:], in1=mean_weights[:], op=ALU.mult)

        def add_means(h):
            nc.vector.tensor_reduce(
                out=den[h][:], in_=row_means[h][:].rearrange("p (s b) -> p b s", s=SLABS), axis=mybir.AxisListType.X, op=ALU.add
            )

        def invert(h):
            nc.vector.reciprocal(out=inv_den[h][:], in_=den[h][:])

        def units_of(r):
            return [u for u in (2 * r, 2 * r + 1) if 0 <= u < UNITS]

        def last_slab(units):
            return [u for u in units if place(u)[1] == SLABS - 1]

        def job_bank(job):
            return (row_banks + sum_banks)[job] if job < 4 else row_banks[job % 2]

        last_round = ROUNDS + MIX_LAG
        jobs_in = {r: [r + 4] for r in range(1, len(turn_jobs) - 4)}
        jobs_in[-1] = [1, 2]
        jobs_in[0] = [3, 4]
        halves_in = {-1: [2], 0: [4, 5]}
        for r in range(1, 11):
            halves_in[r] = [r + 5]
        store_rounds = [r for r in range(last_round) if last_slab(units_of(r - MIX_LAG))]
        widen_round = {}
        for job in reversed(widen_jobs[2:]):
            r = min(i for i in halves_in if job[0] in halves_in[i]) - 1
            while r in store_rounds or r in widen_round:
                r = r - 1
            widen_round[r] = job

        def keep_clock(count, bank):
            for i in range(count):
                nc.tensor.matmul(bank[:, :P], lhsT=identity[:], rhs=identity[:], start=True, stop=True)

        keep_clock(8, turn_banks[0])
        for job in range(3):
            turn_rows(job, job_bank(job))
            if job == 0:
                keep_clock(2, turn_banks[0])
            if job == 0:
                widen(widen_jobs[0])
            empty_turned(job, job_bank(job))
        widen(widen_jobs[1])
        interleave(3)
        interleave(0)
        interleave(1)
        quantize_half(0)
        quantize_half(1)
        quantize_turned(0)
        interleave(2)
        quantize_half(3)

        for r in range(last_round):
            finished = last_slab(units_of(r - 1))
            pair = 2 * place(finished[0])[0] + place(finished[0])[2] // 2 if finished else None

            turning = jobs_in.get(r, [])
            for u in units_of(r):
                scores(u)
            for u in units_of(r - MIX_LAG):
                mix(u)
            if 0 < r < MIX_LAG:
                keep_clock(2, sum_banks[0])
            for u in units_of(r):
                weigh(u)
            for u in units_of(r - 1):
                turn_weights(u)
            for job in turning:
                turn_rows(job, job_bank(job))
                if job == 3:
                    keep_clock(2, turn_banks[0])
            for u in last_slab(units_of(r - MIX_LAG)):
                divide_and_store(u)
            if r in widen_round:
                widen(widen_round[r])

            for job in jobs_in.get(r - 1, []):
                if job < 6:
                    quantize_turned(job)
            for job in jobs_in.get(r - 2, []):
                if job >= 6:
                    quantize_turned(job)
            for half in halves_in.get(r - 1, []):
                quantize_half(half)
            for half in halves_in.get(r, []):
                if half >= SHARED_FROM:
                    interleave_aside(half)
            if finished:
                means(pair)
            for u in units_of(r - 1)[:1]:
                apply_gain(u)
            if finished:
                add_means(pair)
            if r == ROUNDS:
                quantize_gained([UNITS - 2])
            for u in units_of(r - 1)[1:]:
                apply_gain(u)
            for half in halves_in.get(r, []):
                interleave(half)
            if finished:
                invert(pair)
            if 1 <= r <= ROUNDS:
                quantize_gained([u for u in units_of(r - 1) if u != UNITS - 2])

            for job in turning:
                empty_turned(job, job_bank(job))
